import numpy as np, ml_dtypes
CORES = [16,23,24,31,64,71]
N = 6
NB, TK, FT = 4, 32, 4
def setup_inputs(rng):
    return {"x": rng.standard_normal((N, NB, 128, TK), dtype=np.float32).astype(ml_dtypes.bfloat16), "w1": (rng.standard_normal((N, 128, FT * 128), dtype=np.float32) / 8).astype(ml_dtypes.bfloat16), "w2": (rng.standard_normal((N, 128, FT * 128), dtype=np.float32) / np.float32(8 * np.sqrt(FT))).astype(ml_dtypes.bfloat16)}
def setup_inputs_big(rng):
    d = setup_inputs(rng)
    for k in ("x",): d[k] = (d[k].astype(np.float32) * 1048576.0).astype(d[k].dtype)
    return d
def setup_inputs_small(rng):
    d = setup_inputs(rng)
    for k in ("x",): d[k] = (d[k].astype(np.float32) * (1 / 1048576.0)).astype(d[k].dtype)
    return d
def reference(x, w1, w2):
    W1, W2 = w1.astype(np.float64), w2.astype(np.float64)
    a = x[0].astype(np.float64)
    for s in range(N):
        a = sum(np.einsum("kf,bkn->bfn", W2[s][:, 128 * f:128 * f + 128], np.maximum(np.einsum("kf,bkn->bfn", W1[s][:, 128 * f:128 * f + 128], a), 0.0)) for f in range(FT))
    y = np.full(x.shape, np.nan, ml_dtypes.bfloat16)
    y[N - 1] = a.astype(ml_dtypes.bfloat16)
    return {"y": y}

@@ -1,0 +1,205 @@
+from concourse.mybir import AluOpType
+
+N, NB, TK, FT, P = 6, 4, 32, 4, 128
+COLS = NB * TK
+NCH = 2
+CW = COLS // NCH
+BPC = NB // NCH
+HALF = FT * P
+NHB = 6
+NOB = 2
+ACT_ENG = 8
+W_ENG = 16
+MAXP = 3
+
+SCRATCH = {"zero": ("sbuf", [P, CW], "float32")}
+for _s in range(N):
+    SCRATCH["wt%d" % _s] = ("sbuf", [P, 2 * HALF], "bfloat16")
+    SCRATCH["h%d" % _s] = ("sbuf", [P, FT * COLS], "bfloat16")
+for _s in range(N + 1):
+    SCRATCH["a%d" % _s] = ("sbuf", [P, COLS], "bfloat16")
+for _b in range(NHB):
+    SCRATCH["ph%d" % _b] = ("psum", [P, 512], "float32")
+for _b in range(NOB):
+    SCRATCH["po%d" % _b] = ("psum", [P, 512], "float32")
+
+SEMAPHORES = (["ldx%d" % j for j in range(NCH)] + ["ldw0", "ldw1"]
+              + ["wa%d_%d" % (s, i) for s in range(N) for i in range(MAXP)]
+              + ["in%d" % j for j in range(NCH)] + ["rl", "sent", "td", "vd", "zs", "st"])
+
+
+def _plan(cores, topo):
+    n = len(cores)
+    place = list(cores)
+    first = topo.chip(cores[0])
+    nxt = None
+    s = n - 1
+    while s >= 0:
+        ch = topo.chip(cores[s])
+        grp = [r for r in range(n) if topo.chip(cores[r]) == ch]
+        if ch != first:
+            if nxt is None:
+                home = cores[grp[-1]]
+            else:
+                home = [cores[r] for r in reversed(grp) if topo.may_write(cores[r], nxt)][0]
+            for r in grp:
+                place[r] = home
+        nxt = place[grp[0]]
+        s = grp[0] - 1
+    routes = []
+    for s in range(n):
+        if place[s] == cores[s]:
+            routes.append([])
+        else:
+            routes.append([(k * HALF, (k + 1) * HALF, [cores[s], place[s]]) for k in range(2)])
+    return place, routes
+
+
+def _engines(mask, n):
+    on = [b for b in range(mask.bit_length()) if (mask >> b) & 1]
+    n = min(n, len(on))
+    step = len(on) // n
+    return sum(1 << on[i * step] for i in range(n)), n
+
+
+def _send(g, T, topo, src, dst, ap, rsem, n):
+    rid, pid, _ = topo.addr(dst)
+    m, n = _engines(topo.mask(src, dst), n)
+    g.remote_dma(out_ap=ap, in_ap=ap, remote_sem=rsem, local_sem=T.sem.sent, pid=pid, routing_id=rid,
+                 dma_engine_mask=m)
+    return n
+
+
+def rank_program(g, core, T, topo):
+    cores = list(T.cores)
+    rank = T.rank_of(core)
+    place, routes = _plan(cores, topo)
+    mine = [s for s in range(N) if place[s] == core]
+    sem = T.sem
+    sent = 0
+    q = [g.sync, g.scalar]
+
+    def load_x(j):
+        for i in range(BPC):
+            m = j * BPC + i
+            q[i % 2].dma_start(T.a0[:, m * TK:(m + 1) * TK], T.x[m]).then_inc(sem["ldx%d" % j], 16)
+
+    if rank is not None:
+        w = T["wt%d" % rank]
+        if rank == 0:
+            load_x(0)
+        g.sync.dma_start(w[:, 0:HALF], T.w1[:, :]).then_inc(sem.ldw0, 16)
+        g.scalar.dma_start(w[:, HALF:2 * HALF], T.w2[:, :]).then_inc(sem.ldw1, 16)
+        if rank == 0:
+            for j in range(1, NCH):
+                load_x(j)
+
+    g_saw = set()
+    for s in range(N):
+        for i, (c0, c1, path) in enumerate(routes[s]):
+            for k in range(len(path) - 1):
+                if path[k] != core:
+                    continue
+                if k == 0:
+                    for half in range(2):
+                        if c0 < (half + 1) * HALF and c1 > half * HALF and half not in g_saw:
+                            g_saw.add(half)
+                            g.wait_ge(sem["ldw%d" % half], 16)
+                else:
+                    g.wait_ge(sem.rl, _engines(topo.mask(path[k - 1], core), W_ENG)[1])
+                rsem = sem["wa%d_%d" % (s, i)] if k == len(path) - 2 else sem.rl
+                sent += _send(g, T, topo, core, path[k + 1], T["wt%d" % s][:, c0:c1], rsem, W_ENG)
+
+    if mine:
+        g.vector.memset(T.zero[:, :], 0.0).then_inc(sem.zs, 1)
+        g.vector.wait_ge(sem.zs, 1)
+    st = {"td": 0, "vd": 0, "t_saw": 0, "v_saw": 0, "hb": 0, "ob": 0, "rd": {}, "wok": set()}
+    copied = {}
+    stored = 0
+
+    def t_wait_vd(v):
+        if v > st["t_saw"]:
+            g.tensor.wait_ge(sem.vd, v)
+            st["t_saw"] = v
+
+    def v_wait_td(v):
+        if v > st["v_saw"]:
+            g.vector.wait_ge(sem.td, v)
+            st["v_saw"] = v
+
+    def t_wait_w(s, x0, x1):
+        if routes[s]:
+            pieces = [(c0, c1, "wa%d_%d" % (s, i), _engines(topo.mask(path[-2], core), W_ENG)[1])
+                      for i, (c0, c1, path) in enumerate(routes[s])]
+        else:
+            pieces = [(k * HALF, (k + 1) * HALF, "ldw%d" % k, 16) for k in range(2)]
+        for c0, c1, name, cnt in pieces:
+            if c0 < x1 and c1 > x0 and name not in st["wok"]:
+                st["wok"].add(name)
+                g.tensor.wait_ge(sem[name], cnt)
+
+    def unit(s, j):
+        c0, c1 = j * CW, (j + 1) * CW
+        a, h, ws, o = T["a%d" % s], T["h%d" % s], T["wt%d" % s], T["a%d" % (s + 1)]
+        if s == 0:
+            g.tensor.wait_ge(sem["ldx%d" % j], 16 * BPC)
+        elif place[s - 1] == core:
+            t_wait_vd(copied[(s - 1, j)])
+        else:
+            g.tensor.wait_ge(sem["in%d" % j], _engines(topo.mask(place[s - 1], core), ACT_ENG)[1])
+        banks, done1 = [], []
+        for f in range(FT):
+            b = "ph%d" % (st["hb"] % NHB)
+            st["hb"] += 1
+            t_wait_w(s, f * P, (f + 1) * P)
+            t_wait_vd(st["rd"].get(b, 0))
+            g.tensor.matmul(T[b][:, 0:CW], ws[:, f * P:(f + 1) * P], a[:, c0:c1], start=True, stop=True
+                            ).then_inc(sem.td, 1)
+            st["td"] += 1
+            banks.append(b)
+            done1.append(st["td"])
+        relu = []
+        for f in range(FT):
+            v_wait_td(done1[f])
+            g.vector.tensor_tensor(h[:, f * COLS + c0:f * COLS + c1], T[banks[f]][:, 0:CW], T.zero[:, 0:CW],
+                                   AluOpType.max).then_inc(sem.vd, 1)
+            st["vd"] += 1
+            st["rd"][banks[f]] = st["vd"]
+            relu.append(st["vd"])
+        b = "po%d" % (st["ob"] % NOB)
+        st["ob"] += 1
+        t_wait_vd(st["rd"].get(b, 0))
+        for f in range(FT):
+            t_wait_w(s, HALF + f * P, HALF + (f + 1) * P)
+            t_wait_vd(relu[f])
+            mm = g.tensor.matmul(T[b][:, 0:CW], ws[:, HALF + f * P:HALF + (f + 1) * P],
+                                 h[:, f * COLS + c0:f * COLS + c1], start=(f == 0), stop=(f == FT - 1))
+        mm.then_inc(sem.td, 1)
+        st["td"] += 1
+        v_wait_td(st["td"])
+        g.vector.tensor_copy(o[:, c0:c1], T[b][:, 0:CW]).then_inc(sem.vd, 1)
+        st["vd"] += 1
+        st["rd"][b] = st["vd"]
+        copied[(s, j)] = st["vd"]
+
+    for j in range(NCH):
+        if not mine:
+            break
+        for s in mine:
+            unit(s, j)
+        s = mine[-1]
+        if s == N - 1:
+            for i in range(BPC):
+                m = j * BPC + i
+                q[i % 2].wait_ge(sem.vd, copied[(s, j)])
+                q[i % 2].dma_start(T.y[m], T["a%d" % N][:, m * TK:(m + 1) * TK]).then_inc(sem.st, 16)
+                stored += 16
+        else:
+            g.wait_ge(sem.vd, copied[(s, j)])
+            sent += _send(g, T, topo, core, place[s + 1], T["a%d" % (s + 1)][:, j * CW:(j + 1) * CW],
+                          sem["in%d" % j], ACT_ENG)
+
+    if sent:
+        g.wait_ge(sem.sent, sent)
+    if stored:
+        g.wait_ge(sem.st, stored)

@@ -10,7 +10,6 @@ NHB = 6
 NOB = 2
 ACT_ENG = 8
 W_ENG = 16
-MAXP = 3
 
 SCRATCH = {"zero": ("sbuf", [P, CW], "float32")}
 for _s in range(N):
@@ -24,13 +23,13 @@ for _b in range(NOB):
     SCRATCH["po%d" % _b] = ("psum", [P, 512], "float32")
 
 SEMAPHORES = (["ldx%d" % j for j in range(NCH)] + ["ldw0", "ldw1"]
-              + ["wa%d_%d" % (s, i) for s in range(N) for i in range(MAXP)]
-              + ["in%d" % j for j in range(NCH)] + ["rl", "sent", "td", "vd", "zs", "st"])
+              + ["wa%d_%d" % (s, k) for s in range(N) for k in range(2)]
+              + ["in%d" % j for j in range(NCH)] + ["sent", "td", "vd", "zs", "st"])
 
 
 def _plan(cores, topo):
     n = len(cores)
-    place = list(cores)
+    main = list(cores)
     first = topo.chip(cores[0])
     nxt = None
     s = n - 1
@@ -43,16 +42,33 @@ def _plan(cores, topo):
             else:
                 home = [cores[r] for r in reversed(grp) if topo.may_write(cores[r], nxt)][0]
             for r in grp:
-                place[r] = home
-        nxt = place[grp[0]]
+                main[r] = home
+        nxt = main[grp[0]]
         s = grp[0] - 1
-    routes = []
+    side = list(main)
+    nxt = cores[-1]
+    for s in range(n - 1, -1, -1):
+        m = main[s]
+        if m == cores[0] or m == cores[-1]:
+            nxt = side[s]
+            continue
+        if s + 1 < n and main[s + 1] == m:
+            side[s] = side[s + 1]
+            continue
+        idle = [c for c in range(topo.CORES_PER_CHIP * topo.CHIPS)
+                if topo.chip(c) == topo.chip(m) and c not in cores and topo.may_write(c, nxt)]
+        idle.sort(key=lambda c: topo.die(c) == topo.die(m))
+        side[s] = idle[0]
+        nxt = side[s]
+    place = [main] + [side] * (NCH - 1)
+    dests = []
     for s in range(n):
-        if place[s] == cores[s]:
-            routes.append([])
-        else:
-            routes.append([(k * HALF, (k + 1) * HALF, [cores[s], place[s]]) for k in range(2)])
-    return place, routes
+        d = []
+        for j in range(NCH):
+            if place[j][s] != cores[s] and place[j][s] not in d:
+                d.append(place[j][s])
+        dests.append(d)
+    return place, dests
 
 
 def _engines(mask, n):
@@ -73,8 +89,8 @@ def _send(g, T, topo, src, dst, ap, rsem, n):
 def rank_program(g, core, T, topo):
     cores = list(T.cores)
     rank = T.rank_of(core)
-    place, routes = _plan(cores, topo)
-    mine = [s for s in range(N) if place[s] == core]
+    place, dests = _plan(cores, topo)
+    mine = [(s, j) for j in range(NCH) for s in range(N) if place[j][s] == core]
     sem = T.sem
     sent = 0
     q = [g.sync, g.scalar]
@@ -93,22 +109,11 @@ def rank_program(g, core, T, topo):
         if rank == 0:
             for j in range(1, NCH):
                 load_x(j)
-
-    g_saw = set()
-    for s in range(N):
-        for i, (c0, c1, path) in enumerate(routes[s]):
-            for k in range(len(path) - 1):
-                if path[k] != core:
-                    continue
-                if k == 0:
-                    for half in range(2):
-                        if c0 < (half + 1) * HALF and c1 > half * HALF and half not in g_saw:
-                            g_saw.add(half)
-                            g.wait_ge(sem["ldw%d" % half], 16)
-                else:
-                    g.wait_ge(sem.rl, _engines(topo.mask(path[k - 1], core), W_ENG)[1])
-                rsem = sem["wa%d_%d" % (s, i)] if k == len(path) - 2 else sem.rl
-                sent += _send(g, T, topo, core, path[k + 1], T["wt%d" % s][:, c0:c1], rsem, W_ENG)
+        for i, d in enumerate(dests[rank]):
+            for k in range(2):
+                if i == 0:
+                    g.wait_ge(sem["ldw%d" % k], 16)
+                sent += _send(g, T, topo, core, d, w[:, k * HALF:(k + 1) * HALF], sem["wa%d_%d" % (rank, k)], W_ENG)
 
     if mine:
         g.vector.memset(T.zero[:, :], 0.0).then_inc(sem.zs, 1)
@@ -127,31 +132,29 @@ def rank_program(g, core, T, topo):
             g.vector.wait_ge(sem.td, v)
             st["v_saw"] = v
 
-    def t_wait_w(s, x0, x1):
-        if routes[s]:
-            pieces = [(c0, c1, "wa%d_%d" % (s, i), _engines(topo.mask(path[-2], core), W_ENG)[1])
-                      for i, (c0, c1, path) in enumerate(routes[s])]
+    def t_wait_w(s, k):
+        if (s, k) in st["wok"]:
+            return
+        st["wok"].add((s, k))
+        if cores[s] == core:
+            g.tensor.wait_ge(sem["ldw%d" % k], 16)
         else:
-            pieces = [(k * HALF, (k + 1) * HALF, "ldw%d" % k, 16) for k in range(2)]
-        for c0, c1, name, cnt in pieces:
-            if c0 < x1 and c1 > x0 and name not in st["wok"]:
-                st["wok"].add(name)
-                g.tensor.wait_ge(sem[name], cnt)
+            g.tensor.wait_ge(sem["wa%d_%d" % (s, k)], _engines(topo.mask(cores[s], core), W_ENG)[1])
 
     def unit(s, j):
         c0, c1 = j * CW, (j + 1) * CW
         a, h, ws, o = T["a%d" % s], T["h%d" % s], T["wt%d" % s], T["a%d" % (s + 1)]
         if s == 0:
             g.tensor.wait_ge(sem["ldx%d" % j], 16 * BPC)
-        elif place[s - 1] == core:
+        elif place[j][s - 1] == core:
             t_wait_vd(copied[(s - 1, j)])
         else:
-            g.tensor.wait_ge(sem["in%d" % j], _engines(topo.mask(place[s - 1], core), ACT_ENG)[1])
+            g.tensor.wait_ge(sem["in%d" % j], _engines(topo.mask(place[j][s - 1], core), ACT_ENG)[1])
+        t_wait_w(s, 0)
         banks, done1 = [], []
         for f in range(FT):
             b = "ph%d" % (st["hb"] % NHB)
             st["hb"] += 1
-            t_wait_w(s, f * P, (f + 1) * P)
             t_wait_vd(st["rd"].get(b, 0))
             g.tensor.matmul(T[b][:, 0:CW], ws[:, f * P:(f + 1) * P], a[:, c0:c1], start=True, stop=True
                             ).then_inc(sem.td, 1)
@@ -166,11 +169,11 @@ def rank_program(g, core, T, topo):
             st["vd"] += 1
             st["rd"][banks[f]] = st["vd"]
             relu.append(st["vd"])
+        t_wait_w(s, 1)
         b = "po%d" % (st["ob"] % NOB)
         st["ob"] += 1
         t_wait_vd(st["rd"].get(b, 0))
         for f in range(FT):
-            t_wait_w(s, HALF + f * P, HALF + (f + 1) * P)
             t_wait_vd(relu[f])
             mm = g.tensor.matmul(T[b][:, 0:CW], ws[:, HALF + f * P:HALF + (f + 1) * P],
                                  h[:, f * COLS + c0:f * COLS + c1], start=(f == 0), stop=(f == FT - 1))
@@ -182,21 +185,17 @@ def rank_program(g, core, T, topo):
         st["rd"][b] = st["vd"]
         copied[(s, j)] = st["vd"]
 
-    for j in range(NCH):
-        if not mine:
-            break
-        for s in mine:
-            unit(s, j)
-        s = mine[-1]
+    for s, j in mine:
+        unit(s, j)
         if s == N - 1:
             for i in range(BPC):
                 m = j * BPC + i
                 q[i % 2].wait_ge(sem.vd, copied[(s, j)])
                 q[i % 2].dma_start(T.y[m], T["a%d" % N][:, m * TK:(m + 1) * TK]).then_inc(sem.st, 16)
                 stored += 16
-        else:
+        elif place[j][s + 1] != core:
             g.wait_ge(sem.vd, copied[(s, j)])
-            sent += _send(g, T, topo, core, place[s + 1], T["a%d" % (s + 1)][:, j * CW:(j + 1) * CW],
+            sent += _send(g, T, topo, core, place[j][s + 1], T["a%d" % (s + 1)][:, j * CW:(j + 1) * CW],
                           sem["in%d" % j], ACT_ENG)
 
     if sent:

@@ -24,51 +24,29 @@ for _b in range(NOB):
 
 SEMAPHORES = (["ldx%d" % j for j in range(NCH)] + ["ldw0", "ldw1"]
               + ["wa%d_%d" % (s, k) for s in range(N) for k in range(2)]
-              + ["in%d" % j for j in range(NCH)] + ["sent", "td", "vd", "zs", "st"])
+              + ["inp", "sent", "td", "vd", "zs", "st"])
+
+
+def _way(src, dst, k, cores, topo):
+    if topo.may_write(src, dst):
+        return [src, dst]
+    here = [c for c in range(topo.CORES_PER_CHIP * topo.CHIPS)
+            if topo.chip(c) == topo.chip(src) and c != src and topo.may_write(c, dst)]
+    ranks = [c for c in here if c in cores]
+    idle = [c for c in here if c not in cores]
+    idle.sort(key=lambda c: topo.die(c) in [topo.die(r) for r in ranks])
+    via = (ranks + idle) if k == 0 else idle
+    return [src, via[0], dst]
 
 
 def _plan(cores, topo):
-    n = len(cores)
-    main = list(cores)
-    first = topo.chip(cores[0])
-    nxt = None
-    s = n - 1
-    while s >= 0:
-        ch = topo.chip(cores[s])
-        grp = [r for r in range(n) if topo.chip(cores[r]) == ch]
-        if ch != first:
-            if nxt is None:
-                home = cores[grp[-1]]
-            else:
-                home = [cores[r] for r in reversed(grp) if topo.may_write(cores[r], nxt)][0]
-            for r in grp:
-                main[r] = home
-        nxt = main[grp[0]]
-        s = grp[0] - 1
-    side = list(main)
-    nxt = cores[-1]
-    for s in range(n - 1, -1, -1):
-        m = main[s]
-        if m == cores[0] or m == cores[-1]:
-            nxt = side[s]
-            continue
-        if s + 1 < n and main[s + 1] == m:
-            side[s] = side[s + 1]
-            continue
-        idle = [c for c in range(topo.CORES_PER_CHIP * topo.CHIPS)
-                if topo.chip(c) == topo.chip(m) and c not in cores and topo.may_write(c, nxt)]
-        idle.sort(key=lambda c: topo.die(c) == topo.die(m))
-        side[s] = idle[0]
-        nxt = side[s]
-    place = [main] + [side] * (NCH - 1)
-    dests = []
-    for s in range(n):
-        d = []
-        for j in range(NCH):
-            if place[j][s] != cores[s] and place[j][s] not in d:
-                d.append(place[j][s])
-        dests.append(d)
-    return place, dests
+    place = [cores[0] if topo.chip(c) == topo.chip(cores[0]) else cores[-1] for c in cores]
+    routes = {}
+    for s in range(len(cores)):
+        if cores[s] != place[s]:
+            for k in range(2):
+                routes[(s, k)] = _way(cores[s], place[s], k, cores, topo)
+    return place, routes
 
 
 def _engines(mask, n):
@@ -89,36 +67,42 @@ def _send(g, T, topo, src, dst, ap, rsem, n):
 def rank_program(g, core, T, topo):
     cores = list(T.cores)
     rank = T.rank_of(core)
-    place, dests = _plan(cores, topo)
-    mine = [(s, j) for j in range(NCH) for s in range(N) if place[j][s] == core]
+    place, routes = _plan(cores, topo)
+    mine = [s for s in range(N) if place[s] == core]
     sem = T.sem
     sent = 0
     q = [g.sync, g.scalar]
 
-    def load_x(j):
-        for i in range(BPC):
-            m = j * BPC + i
-            q[i % 2].dma_start(T.a0[:, m * TK:(m + 1) * TK], T.x[m]).then_inc(sem["ldx%d" % j], 16)
+    def load_x(m, qi):
+        q[qi].dma_start(T.a0[:, m * TK:(m + 1) * TK], T.x[m]).then_inc(sem["ldx%d" % (m // BPC)], 16)
 
     if rank is not None:
         w = T["wt%d" % rank]
         if rank == 0:
-            load_x(0)
+            load_x(0, 0)
+            load_x(1, 1)
+            load_x(2, 1)
         g.sync.dma_start(w[:, 0:HALF], T.w1[:, :]).then_inc(sem.ldw0, 16)
         g.scalar.dma_start(w[:, HALF:2 * HALF], T.w2[:, :]).then_inc(sem.ldw1, 16)
         if rank == 0:
-            for j in range(1, NCH):
-                load_x(j)
-        for i, d in enumerate(dests[rank]):
-            for k in range(2):
-                if i == 0:
-                    g.wait_ge(sem["ldw%d" % k], 16)
-                sent += _send(g, T, topo, core, d, w[:, k * HALF:(k + 1) * HALF], sem["wa%d_%d" % (rank, k)], W_ENG)
+            load_x(3, 0)
+
+    jobs = [(s, k, routes[(s, k)].index(core)) for (s, k) in sorted(routes) if core in routes[(s, k)][:-1]]
+    jobs.sort(key=lambda t: 1 if t[2] > 0 else 2 * t[1])
+    for s, k, i in jobs:
+        path = routes[(s, k)]
+        if i == 0:
+            g.wait_ge(sem["ldw%d" % k], 16)
+        else:
+            g.wait_ge(sem["wa%d_%d" % (s, k)], _engines(topo.mask(path[i - 1], core), W_ENG)[1])
+        sent += _send(g, T, topo, core, path[i + 1], T["wt%d" % s][:, k * HALF:(k + 1) * HALF],
+                      sem["wa%d_%d" % (s, k)], W_ENG)
 
     if mine:
         g.vector.memset(T.zero[:, :], 0.0).then_inc(sem.zs, 1)
         g.vector.wait_ge(sem.zs, 1)
-    st = {"td": 0, "vd": 0, "t_saw": 0, "v_saw": 0, "hb": 0, "ob": 0, "rd": {}, "wok": set()}
+    st = {"td": 0, "vd": 0, "t_saw": 0, "v_saw": 0, "hb": 0, "ob": 0, "rd": {}, "wok": set(), "got": False}
+    relu = {}
     copied = {}
     stored = 0
 
@@ -139,17 +123,18 @@ def rank_program(g, core, T, topo):
         if cores[s] == core:
             g.tensor.wait_ge(sem["ldw%d" % k], 16)
         else:
-            g.tensor.wait_ge(sem["wa%d_%d" % (s, k)], _engines(topo.mask(cores[s], core), W_ENG)[1])
+            g.tensor.wait_ge(sem["wa%d_%d" % (s, k)], _engines(topo.mask(routes[(s, k)][-2], core), W_ENG)[1])
 
-    def unit(s, j):
+    def first_half(s, j):
         c0, c1 = j * CW, (j + 1) * CW
-        a, h, ws, o = T["a%d" % s], T["h%d" % s], T["wt%d" % s], T["a%d" % (s + 1)]
+        a, h, ws = T["a%d" % s], T["h%d" % s], T["wt%d" % s]
         if s == 0:
             g.tensor.wait_ge(sem["ldx%d" % j], 16 * BPC)
-        elif place[j][s - 1] == core:
+        elif place[s - 1] == core:
             t_wait_vd(copied[(s - 1, j)])
-        else:
-            g.tensor.wait_ge(sem["in%d" % j], _engines(topo.mask(place[j][s - 1], core), ACT_ENG)[1])
+        elif not st["got"]:
+            g.tensor.wait_ge(sem.inp, _engines(topo.mask(place[s - 1], core), ACT_ENG)[1])
+            st["got"] = True
         t_wait_w(s, 0)
         banks, done1 = [], []
         for f in range(FT):
@@ -161,20 +146,24 @@ def rank_program(g, core, T, topo):
             st["td"] += 1
             banks.append(b)
             done1.append(st["td"])
-        relu = []
+        relu[(s, j)] = []
         for f in range(FT):
             v_wait_td(done1[f])
             g.vector.tensor_tensor(h[:, f * COLS + c0:f * COLS + c1], T[banks[f]][:, 0:CW], T.zero[:, 0:CW],
                                    AluOpType.max).then_inc(sem.vd, 1)
             st["vd"] += 1
             st["rd"][banks[f]] = st["vd"]
-            relu.append(st["vd"])
+            relu[(s, j)].append(st["vd"])
+
+    def second_half(s, j):
+        c0, c1 = j * CW, (j + 1) * CW
+        h, ws, o = T["h%d" % s], T["wt%d" % s], T["a%d" % (s + 1)]
         t_wait_w(s, 1)
         b = "po%d" % (st["ob"] % NOB)
         st["ob"] += 1
         t_wait_vd(st["rd"].get(b, 0))
         for f in range(FT):
-            t_wait_vd(relu[f])
+            t_wait_vd(relu[(s, j)][f])
             mm = g.tensor.matmul(T[b][:, 0:CW], ws[:, HALF + f * P:HALF + (f + 1) * P],
                                  h[:, f * COLS + c0:f * COLS + c1], start=(f == 0), stop=(f == FT - 1))
         mm.then_inc(sem.td, 1)
@@ -185,18 +174,20 @@ def rank_program(g, core, T, topo):
         st["rd"][b] = st["vd"]
         copied[(s, j)] = st["vd"]
 
-    for s, j in mine:
-        unit(s, j)
-        if s == N - 1:
-            for i in range(BPC):
-                m = j * BPC + i
-                q[i % 2].wait_ge(sem.vd, copied[(s, j)])
-                q[i % 2].dma_start(T.y[m], T["a%d" % N][:, m * TK:(m + 1) * TK]).then_inc(sem.st, 16)
-                stored += 16
-        elif place[j][s + 1] != core:
-            g.wait_ge(sem.vd, copied[(s, j)])
-            sent += _send(g, T, topo, core, place[j][s + 1], T["a%d" % (s + 1)][:, j * CW:(j + 1) * CW],
-                          sem["in%d" % j], ACT_ENG)
+    for s in mine:
+        for j in range(NCH):
+            first_half(s, j)
+        for j in range(NCH):
+            second_half(s, j)
+            if s == N - 1:
+                for i in range(BPC):
+                    m = j * BPC + i
+                    q[i % 2].wait_ge(sem.vd, copied[(s, j)])
+                    q[i % 2].dma_start(T.y[m], T["a%d" % N][:, m * TK:(m + 1) * TK]).then_inc(sem.st, 16)
+                    stored += 16
+        if s < N - 1 and place[s + 1] != core:
+            g.wait_ge(sem.vd, copied[(s, NCH - 1)])
+            sent += _send(g, T, topo, core, place[s + 1], T["a%d" % (s + 1)][:, :], sem.inp, ACT_ENG)
 
     if sent:
         g.wait_ge(sem.sent, sent)

@@ -6,10 +6,9 @@ NCH = 2
 CW = COLS // NCH
 BPC = NB // NCH
 HALF = FT * P
-NHB = 6
-NOB = 2
 ACT_ENG = 8
 W_ENG = 16
+LDW = 32
 
 SCRATCH = {"zero": ("sbuf", [P, CW], "float32")}
 for _s in range(N):
@@ -17,10 +16,8 @@ for _s in range(N):
     SCRATCH["h%d" % _s] = ("sbuf", [P, FT * COLS], "bfloat16")
 for _s in range(N + 1):
     SCRATCH["a%d" % _s] = ("sbuf", [P, COLS], "bfloat16")
-for _b in range(NHB):
+for _b in range(NCH * FT):
     SCRATCH["ph%d" % _b] = ("psum", [P, 512], "float32")
-for _b in range(NOB):
-    SCRATCH["po%d" % _b] = ("psum", [P, 512], "float32")
 
 SEMAPHORES = (["ldx%d" % j for j in range(NCH)] + ["ldw0", "ldw1"]
               + ["wa%d_%d" % (s, k) for s in range(N) for k in range(2)]
@@ -73,26 +70,32 @@ def rank_program(g, core, T, topo):
     sent = 0
     q = [g.sync, g.scalar]
 
-    def load_x(m, qi):
-        q[qi].dma_start(T.a0[:, m * TK:(m + 1) * TK], T.x[m]).then_inc(sem["ldx%d" % (m // BPC)], 16)
+    def load_x(j):
+        for i in range(BPC):
+            m = j * BPC + i
+            q[i % 2].dma_start(T.a0[:, m * TK:(m + 1) * TK], T.x[m]).then_inc(sem["ldx%d" % j], 16)
+
+    def load_w(k, src):
+        for i in range(2):
+            r0, r1 = i * (P // 2), (i + 1) * (P // 2)
+            q[i].dma_start(T["wt%d" % rank][r0:r1, k * HALF:(k + 1) * HALF], src[r0:r1, :]
+                           ).then_inc(sem["ldw%d" % k], 16)
 
     if rank is not None:
-        w = T["wt%d" % rank]
         if rank == 0:
-            load_x(0, 0)
-            load_x(1, 1)
-            load_x(2, 1)
-        g.sync.dma_start(w[:, 0:HALF], T.w1[:, :]).then_inc(sem.ldw0, 16)
-        g.scalar.dma_start(w[:, HALF:2 * HALF], T.w2[:, :]).then_inc(sem.ldw1, 16)
+            load_x(0)
+        load_w(0, T.w1)
         if rank == 0:
-            load_x(3, 0)
+            for j in range(1, NCH):
+                load_x(j)
+        load_w(1, T.w2)
 
     jobs = [(s, k, routes[(s, k)].index(core)) for (s, k) in sorted(routes) if core in routes[(s, k)][:-1]]
     jobs.sort(key=lambda t: 1 if t[2] > 0 else 2 * t[1])
     for s, k, i in jobs:
         path = routes[(s, k)]
         if i == 0:
-            g.wait_ge(sem["ldw%d" % k], 16)
+            g.wait_ge(sem["ldw%d" % k], LDW)
         else:
             g.wait_ge(sem["wa%d_%d" % (s, k)], _engines(topo.mask(path[i - 1], core), W_ENG)[1])
         sent += _send(g, T, topo, core, path[i + 1], T["wt%d" % s][:, k * HALF:(k + 1) * HALF],
@@ -101,7 +104,7 @@ def rank_program(g, core, T, topo):
     if mine:
         g.vector.memset(T.zero[:, :], 0.0).then_inc(sem.zs, 1)
         g.vector.wait_ge(sem.zs, 1)
-    st = {"td": 0, "vd": 0, "t_saw": 0, "v_saw": 0, "hb": 0, "ob": 0, "rd": {}, "wok": set(), "got": False}
+    st = {"td": 0, "vd": 0, "t_saw": 0, "v_saw": 0, "rd": {}, "wok": set(), "got": False}
     relu = {}
     copied = {}
     stored = 0
@@ -121,7 +124,7 @@ def rank_program(g, core, T, topo):
             return
         st["wok"].add((s, k))
         if cores[s] == core:
-            g.tensor.wait_ge(sem["ldw%d" % k], 16)
+            g.tensor.wait_ge(sem["ldw%d" % k], LDW)
         else:
             g.tensor.wait_ge(sem["wa%d_%d" % (s, k)], _engines(topo.mask(routes[(s, k)][-2], core), W_ENG)[1])
 
@@ -138,8 +141,7 @@ def rank_program(g, core, T, topo):
         t_wait_w(s, 0)
         banks, done1 = [], []
         for f in range(FT):
-            b = "ph%d" % (st["hb"] % NHB)
-            st["hb"] += 1
+            b = "ph%d" % (j * FT + f)
             t_wait_vd(st["rd"].get(b, 0))
             g.tensor.matmul(T[b][:, 0:CW], ws[:, f * P:(f + 1) * P], a[:, c0:c1], start=True, stop=True
                             ).then_inc(sem.td, 1)
@@ -159,8 +161,7 @@ def rank_program(g, core, T, topo):
         c0, c1 = j * CW, (j + 1) * CW
         h, ws, o = T["h%d" % s], T["wt%d" % s], T["a%d" % (s + 1)]
         t_wait_w(s, 1)
-        b = "po%d" % (st["ob"] % NOB)
-        st["ob"] += 1
+        b = "ph%d" % (j * FT)
         t_wait_vd(st["rd"].get(b, 0))
         for f in range(FT):
             t_wait_vd(relu[(s, j)][f])

from concourse.mybir import AluOpType

N, NB, TK, FT, P = 6, 4, 32, 4, 128
COLS = NB * TK
NCH = 2
CW = COLS // NCH
BPC = NB // NCH
HALF = FT * P
ACT_ENG = 8
W_ENG = 16
LDW = 32

SCRATCH = {"zero": ("sbuf", [P, CW], "float32")}
for _s in range(N):
    SCRATCH["wt%d" % _s] = ("sbuf", [P, 2 * HALF], "bfloat16")
    SCRATCH["h%d" % _s] = ("sbuf", [P, FT * COLS], "bfloat16")
for _s in range(N + 1):
    SCRATCH["a%d" % _s] = ("sbuf", [P, COLS], "bfloat16")
for _b in range(NCH * FT):
    SCRATCH["ph%d" % _b] = ("psum", [P, 512], "float32")

SEMAPHORES = (["ldx%d" % j for j in range(NCH)] + ["ldw0", "ldw1"]
              + ["wa%d_%d" % (s, k) for s in range(N) for k in range(2)]
              + ["inp", "sent", "td", "vd", "zs", "st"])


def _way(src, dst, k, cores, topo):
    if topo.may_write(src, dst):
        return [src, dst]
    here = [c for c in range(topo.CORES_PER_CHIP * topo.CHIPS)
            if topo.chip(c) == topo.chip(src) and c != src and topo.may_write(c, dst)]
    ranks = [c for c in here if c in cores]
    idle = [c for c in here if c not in cores]
    idle.sort(key=lambda c: topo.die(c) in [topo.die(r) for r in ranks])
    via = (ranks + idle) if k == 0 else idle
    return [src, via[0], dst]


def _plan(cores, topo):
    place = [cores[0] if topo.chip(c) == topo.chip(cores[0]) else cores[-1] for c in cores]
    routes = {}
    for s in range(len(cores)):
        if cores[s] != place[s]:
            for k in range(2):
                routes[(s, k)] = _way(cores[s], place[s], k, cores, topo)
    return place, routes


def _engines(mask, n):
    on = [b for b in range(mask.bit_length()) if (mask >> b) & 1]
    n = min(n, len(on))
    step = len(on) // n
    return sum(1 << on[i * step] for i in range(n)), n


def _send(g, T, topo, src, dst, ap, rsem, n):
    rid, pid, _ = topo.addr(dst)
    m, n = _engines(topo.mask(src, dst), n)
    g.remote_dma(out_ap=ap, in_ap=ap, remote_sem=rsem, local_sem=T.sem.sent, pid=pid, routing_id=rid,
                 dma_engine_mask=m)
    return n


def rank_program(g, core, T, topo):
    cores = list(T.cores)
    rank = T.rank_of(core)
    place, routes = _plan(cores, topo)
    mine = [s for s in range(N) if place[s] == core]
    sem = T.sem
    sent = 0
    q = [g.sync, g.scalar]

    def load_x(j):
        for i in range(BPC):
            m = j * BPC + i
            q[i % 2].dma_start(T.a0[:, m * TK:(m + 1) * TK], T.x[m]).then_inc(sem["ldx%d" % j], 16)

    def load_w(k, src):
        for i in range(2):
            r0, r1 = i * (P // 2), (i + 1) * (P // 2)
            q[i].dma_start(T["wt%d" % rank][r0:r1, k * HALF:(k + 1) * HALF], src[r0:r1, :]
                           ).then_inc(sem["ldw%d" % k], 16)

    if rank is not None:
        if rank == 0:
            load_x(0)
        load_w(0, T.w1)
        if rank == 0:
            for j in range(1, NCH):
                load_x(j)
        load_w(1, T.w2)

    jobs = [(s, k, routes[(s, k)].index(core)) for (s, k) in sorted(routes) if core in routes[(s, k)][:-1]]
    jobs.sort(key=lambda t: 1 if t[2] > 0 else 2 * t[1])
    for s, k, i in jobs:
        path = routes[(s, k)]
        if i == 0:
            g.wait_ge(sem["ldw%d" % k], LDW)
        else:
            g.wait_ge(sem["wa%d_%d" % (s, k)], _engines(topo.mask(path[i - 1], core), W_ENG)[1])
        sent += _send(g, T, topo, core, path[i + 1], T["wt%d" % s][:, k * HALF:(k + 1) * HALF],
                      sem["wa%d_%d" % (s, k)], W_ENG)

    if mine:
        g.vector.memset(T.zero[:, :], 0.0).then_inc(sem.zs, 1)
        g.vector.wait_ge(sem.zs, 1)
    st = {"td": 0, "vd": 0, "t_saw": 0, "v_saw": 0, "rd": {}, "wok": set(), "got": False}
    relu = {}
    copied = {}
    stored = 0

    def t_wait_vd(v):
        if v > st["t_saw"]:
            g.tensor.wait_ge(sem.vd, v)
            st["t_saw"] = v

    def v_wait_td(v):
        if v > st["v_saw"]:
            g.vector.wait_ge(sem.td, v)
            st["v_saw"] = v

    def t_wait_w(s, k):
        if (s, k) in st["wok"]:
            return
        st["wok"].add((s, k))
        if cores[s] == core:
            g.tensor.wait_ge(sem["ldw%d" % k], LDW)
        else:
            g.tensor.wait_ge(sem["wa%d_%d" % (s, k)], _engines(topo.mask(routes[(s, k)][-2], core), W_ENG)[1])

    def first_half(s, j):
        c0, c1 = j * CW, (j + 1) * CW
        a, h, ws = T["a%d" % s], T["h%d" % s], T["wt%d" % s]
        if s == 0:
            g.tensor.wait_ge(sem["ldx%d" % j], 16 * BPC)
        elif place[s - 1] == core:
            t_wait_vd(copied[(s - 1, j)])
        elif not st["got"]:
            g.tensor.wait_ge(sem.inp, _engines(topo.mask(place[s - 1], core), ACT_ENG)[1])
            st["got"] = True
        t_wait_w(s, 0)
        banks, done1 = [], []
        for f in range(FT):
            b = "ph%d" % (j * FT + f)
            t_wait_vd(st["rd"].get(b, 0))
            g.tensor.matmul(T[b][:, 0:CW], ws[:, f * P:(f + 1) * P], a[:, c0:c1], start=True, stop=True
                            ).then_inc(sem.td, 1)
            st["td"] += 1
            banks.append(b)
            done1.append(st["td"])
        relu[(s, j)] = []
        for f in range(FT):
            v_wait_td(done1[f])
            g.vector.tensor_tensor(h[:, f * COLS + c0:f * COLS + c1], T[banks[f]][:, 0:CW], T.zero[:, 0:CW],
                                   AluOpType.max).then_inc(sem.vd, 1)
            st["vd"] += 1
            st["rd"][banks[f]] = st["vd"]
            relu[(s, j)].append(st["vd"])

    def second_half(s, j):
        c0, c1 = j * CW, (j + 1) * CW
        h, ws, o = T["h%d" % s], T["wt%d" % s], T["a%d" % (s + 1)]
        t_wait_w(s, 1)
        b = "ph%d" % (j * FT)
        t_wait_vd(st["rd"].get(b, 0))
        for f in range(FT):
            t_wait_vd(relu[(s, j)][f])
            mm = g.tensor.matmul(T[b][:, 0:CW], ws[:, HALF + f * P:HALF + (f + 1) * P],
                                 h[:, f * COLS + c0:f * COLS + c1], start=(f == 0), stop=(f == FT - 1))
        mm.then_inc(sem.td, 1)
        st["td"] += 1
        v_wait_td(st["td"])
        g.vector.tensor_copy(o[:, c0:c1], T[b][:, 0:CW]).then_inc(sem.vd, 1)
        st["vd"] += 1
        st["rd"][b] = st["vd"]
        copied[(s, j)] = st["vd"]

    for s in mine:
        for j in range(NCH):
            first_half(s, j)
        for j in range(NCH):
            second_half(s, j)
            if s == N - 1:
                for i in range(BPC):
                    m = j * BPC + i
                    q[i % 2].wait_ge(sem.vd, copied[(s, j)])
                    q[i % 2].dma_start(T.y[m], T["a%d" % N][:, m * TK:(m + 1) * TK]).then_inc(sem.st, 16)
                    stored += 16
        if s < N - 1 and place[s + 1] != core:
            g.wait_ge(sem.vd, copied[(s, NCH - 1)])
            sent += _send(g, T, topo, core, place[s + 1], T["a%d" % (s + 1)][:, :], sem.inp, ACT_ENG)

    if sent:
        g.wait_ge(sem.sent, sent)
    if stored:
        g.wait_ge(sem.st, stored)
